import numpy as np
import ml_dtypes


def mxq(x, axis, fmt="e4m3"):
    dtype, down = {"e4m3": (ml_dtypes.float8_e4m3fn, 7), "e5m2": (ml_dtypes.float8_e5m2, 14)}[fmt]
    v = np.moveaxis(np.asarray(x, np.float32).astype(ml_dtypes.bfloat16).astype(np.float64), axis, -1)
    blocks = v.reshape(v.shape[:-1] + (-1, 32))
    amax = np.abs(blocks).max(-1, keepdims=True)
    byte = np.maximum(np.where(amax > 0, np.frexp(amax)[1] - 1 + 127, 0) - down, 1)
    scale = np.exp2(byte - 127.0)
    codes = (blocks / scale).astype(np.float32).astype(dtype).astype(np.float64)
    return np.moveaxis((codes * scale).reshape(v.shape), -1, axis)


WIDE = False


def mx_kscale(k):
    if not WIDE:
        return np.ones(k)
    levels = np.array([10, -10, 5, -5, 0])
    if k % 512:
        return np.exp2(np.random.permutation(np.resize(levels, k // 32))).repeat(32)
    a = np.empty((k // 512, 16))
    for p in range(k // 512):
        a[p, :8] = np.random.permutation(np.resize(levels, 8))
        for g in range(8):
            far = levels[np.abs(levels - a[p, g]) >= 10]
            a[p, g + 8] = far[np.random.randint(len(far))]
    return np.exp2(a.ravel()).repeat(32)


def f64(x):
    return np.asarray(x).astype(np.float64)


def striped(idx):
    return np.tile(idx.reshape(-1, 16).T, (8, 1)).astype(np.uint16)


def unstriped(offs):
    return offs[:16].T.reshape(-1).astype(np.int64)


def relu(v):
    return np.maximum(v, 0.0)


K, T, S, H, N, U = 512, 2048, 512, 512, 256, 1024


def setup_inputs():
    n = np.random.standard_normal
    s = mx_kscale(K)[:, None]
    u = mx_kscale(H)
    return {
        "xT": (n((K, T)) * s).astype(np.float32),
        "w1": (n((K, H)) / np.sqrt(K) / s * u).astype(np.float32),
        "w2": (n((H, N)) / np.sqrt(H) / u[:, None]).astype(np.float32),
        "skip": (n((H, U)) * u[:, None]).astype(np.float32),
        "offs": striped(np.random.permutation(T)[:S]),
        "cell": striped(np.random.permutation(U)[:S]),
    }


def reference(xT, w1, w2, skip, offs, cell):
    xq = mxq(f64(xT)[:, unstriped(offs)], 0, "e4m3")
    up = np.zeros((H, U))
    up[:, unstriped(cell)] = relu(mxq(f64(w1), 0, "e4m3").T @ xq)
    z = up + f64(skip)
    return mxq(f64(w2), 0, "e4m3").T @ mxq(z, 0, "e4m3")

@@ -1,0 +1,154 @@
+from contextlib import ExitStack
+
+import concourse.mybir as mybir
+
+K, T, S, H, N, U = 512, 2048, 512, 512, 256, 1024
+FLOPS = 2 * K * H * S + 2 * H * N * U
+
+F32 = mybir.dt.float32
+BF16 = mybir.dt.bfloat16
+U32 = mybir.dt.uint32
+U16 = mybir.dt.uint16
+U8 = mybir.dt.uint8
+FP8X4 = mybir.dt.float8_e4m3fn_x4
+RELU = mybir.ActivationFunctionType.Relu
+ADD = mybir.AluOpType.add
+
+P = 128
+PACK = 4
+HALF = S // 2
+LIST_COLS = HALF // 16
+CHUNK = 256
+RUN = 4
+
+
+def tile_picked_unet_relu_e_kernel(tc, xT, w1, w2, skip, offs, cell, out):
+    nc = tc.nc
+
+    def quantize(codes, scales, grouped):
+        nc.vector.quantize_mx(out=codes.bitcast(FP8X4), scales=scales, in_=grouped)
+
+    def product(acc, w_codes, w_scales, v_codes, v_scales):
+        nc.tensor.matmul_mx(out=acc, lhsT=w_codes.bitcast(FP8X4), lhsT_scale=w_scales,
+                            rhs=v_codes.bitcast(FP8X4), rhs_scale=v_scales, start=True, stop=True)
+
+    with ExitStack() as ctx:
+        keep = ctx.enter_context(tc.tile_pool(name="keep", bufs=1))
+        psum = ctx.enter_context(tc.psum_pool(name="psum", bufs=8))
+
+        offs_sb = keep.tile([P, S // 16], U16, name="offs_sb")
+        cell_sb = keep.tile([P, S // 16], U16, name="cell_sb")
+        w1_raw = keep.tile([P, PACK, H], F32, name="w1_raw")
+        w2_raw = keep.tile([P, PACK, N], F32, name="w2_raw")
+        x_rows = [keep.tile([P, T], F32, name=f"x_rows{j}") for j in range(PACK)]
+        skip_rows = [keep.tile([P, U], F32, name=f"skip_rows{t}") for t in range(PACK)]
+        x_view = xT.rearrange("(p j) w -> j p w", j=PACK)
+        skip_view = skip.rearrange("(p t) v -> t p v", t=PACK)
+
+        nc.sync.dma_start(w1_raw[:], w1.rearrange("(p j) c -> p j c", j=PACK))
+        nc.sync.dma_start(offs_sb[:], offs)
+        for j in range(PACK):
+            nc.sync.dma_start(x_rows[j][:], x_view[j])
+        nc.sync.dma_start(cell_sb[:], cell)
+        nc.sync.dma_start(w2_raw[:], w2.rearrange("(p j) c -> p j c", j=PACK))
+        for t in range(PACK):
+            nc.sync.dma_start(skip_rows[t][:], skip_view[t])
+
+        up = [keep.tile([P, U], F32, name=f"up{t}") for t in range(PACK)]
+        for t in range(PACK):
+            nc.vector.memset(up[t][:], 0.0)
+
+        w1_grouped = keep.tile([P, PACK * H], BF16, name="w1_grouped", align_bytes=64)
+        w1_codes = keep.tile([P, H], U32, name="w1_codes", align_bytes=64)
+        w1_scales = keep.tile([P, H], U8, name="w1_scales", align_bytes=64)
+        nc.scalar.copy(out=w1_grouped[:].rearrange("p (t m j) -> p t m j", t=PACK, j=PACK),
+                       in_=w1_raw[:].rearrange("p j (m t) -> p t m j", t=PACK))
+        quantize(w1_codes[:], w1_scales[:], w1_grouped[:])
+
+        x_grouped = [keep.tile([P, HALF, PACK], BF16, name=f"x_grouped{a}", align_bytes=64) for a in range(2)]
+        x_codes = keep.tile([P, S], U32, name="x_codes", align_bytes=64)
+        x_scales = keep.tile([P, S], U8, name="x_scales", align_bytes=64)
+        halves = [slice(a * HALF, (a + 1) * HALF) for a in range(2)]
+        list_halves = [slice(a * LIST_COLS, (a + 1) * LIST_COLS) for a in range(2)]
+        for j in range(PACK):
+            for a in range(2):
+                nc.vector.tensor_copy(x_grouped[a][:, :, j], x_rows[j][:].indirect(offs_sb[:, list_halves[a]]))
+                if j == PACK - 1:
+                    quantize(x_codes[:, halves[a]], x_scales[:, halves[a]],
+                             x_grouped[a][:].rearrange("p s j -> p (s j)"))
+
+        w2_grouped = keep.tile([P, N, PACK], BF16, name="w2_grouped", align_bytes=64)
+        w2_codes = keep.tile([P, N], U32, name="w2_codes", align_bytes=64)
+        w2_scales = keep.tile([P, N], U8, name="w2_scales", align_bytes=64)
+
+        pieces = [(0, 0, 1), (1, 0, 1), (0, 1, 2), (1, 1, 2), (2, 0, 2), (3, 0, 2)]
+        h_sb = []
+        for n, (t, a, b) in enumerate(pieces):
+            width = (b - a) * HALF
+            cols = slice(a * HALF, b * HALF)
+            rows = slice(t * P, (t + 1) * P)
+            acc = psum.tile([P, width], F32, name="acc", tag="bank")
+            product(acc[:], w1_codes[:, rows], w1_scales[:, rows], x_codes[:, cols], x_scales[:, cols])
+            h = keep.tile([P, width], F32, name=f"h{n}")
+            nc.scalar.activation(h[:], acc[:], RELU)
+            h_sb.append(h)
+
+        nc.scalar.copy(out=w2_grouped[:], in_=w2_raw[:].rearrange("p j c -> p c j"))
+
+        z = keep.tile([P, PACK, U], BF16, name="z")
+        for n, (t, a, b) in enumerate(pieces):
+            nc.vector.tensor_copy(up[t][:].indirect(cell_sb[:, a * LIST_COLS : b * LIST_COLS]), h_sb[n][:])
+            if b == 2 and t < PACK - 1:
+                nc.gpsimd.tensor_tensor(z[:, t, :], up[t][:], skip_rows[t][:], ADD)
+            if t == 2:
+                quantize(w2_codes[:], w2_scales[:], w2_grouped[:].rearrange("p c j -> p (c j)"))
+
+        chunks = U // CHUNK
+        z_grouped = [keep.tile([P, CHUNK, PACK], BF16, name=f"z_grouped{c}", align_bytes=64) for c in range(chunks)]
+        z_codes = [keep.tile([P, CHUNK], U32, name=f"z_codes{c}", align_bytes=64) for c in range(chunks)]
+        z_scales = [keep.tile([P, CHUNK], U8, name=f"z_scales{c}", align_bytes=64) for c in range(chunks)]
+        out_view = out.rearrange("(g p) v -> p g v", p=P)
+
+        def cells(c):
+            return slice(c * CHUNK, (c + 1) * CHUNK)
+
+        def add_last(c):
+            t = PACK - 1
+            nc.vector.tensor_tensor(z[:, t, cells(c)], up[t][:, cells(c)], skip_rows[t][:, cells(c)], ADD)
+
+        def interleave(copy, c):
+            copy(out=z_grouped[c][:].rearrange("p (c i) t -> p c t i", i=RUN),
+                 in_=z[:, :, cells(c)].rearrange("p t (c i) -> p c t i", i=RUN))
+
+        def finish(c):
+            quantize(z_codes[c][:], z_scales[c][:], z_grouped[c][:].rearrange("p v t -> p (v t)"))
+            acc = psum.tile([P, N // P, CHUNK], F32, name="acc", tag="bank")
+            for g in range(N // P):
+                rows = slice(g * P, (g + 1) * P)
+                product(acc[:, g, :], w2_codes[:, rows], w2_scales[:, rows], z_codes[c][:], z_scales[c][:])
+            result = keep.tile([P, N // P, CHUNK], F32, name=f"result{c}")
+            nc.scalar.copy(out=result[:], in_=acc[:])
+            nc.sync.dma_start(out_view[:, :, cells(c)], result[:])
+
+        def finish_last(c):
+            quantize(z_codes[c][:], z_scales[c][:], z_grouped[c][:].rearrange("p v t -> p (v t)"))
+            for g, copy in enumerate((nc.scalar.copy, nc.vector.tensor_copy)):
+                rows = slice(g * P, (g + 1) * P)
+                acc = psum.tile([P, CHUNK], F32, name="acc", tag="bank")
+                product(acc[:], w2_codes[:, rows], w2_scales[:, rows], z_codes[c][:], z_scales[c][:])
+                result = keep.tile([P, CHUNK], F32, name=f"last_result{g}")
+                copy(out=result[:], in_=acc[:])
+                nc.sync.dma_start(out_view[:, g, cells(c)], result[:])
+
+        add_last(0)
+        interleave(nc.scalar.copy, 0)
+        add_last(1)
+        add_last(3)
+        interleave(nc.scalar.copy, 3)
+        add_last(2)
+        interleave(nc.vector.tensor_copy, 1)
+        finish(0)
+        finish(1)
+        interleave(nc.vector.tensor_copy, 2)
+        finish(3)
+        finish_last(2)

@@ -1,6 +1,7 @@
 from contextlib import ExitStack
 
 import concourse.mybir as mybir
+from concourse.masks import make_identity
 
 K, T, S, H, N, U = 512, 2048, 512, 512, 256, 1024
 FLOPS = 2 * K * H * S + 2 * H * N * U
@@ -54,6 +55,11 @@ def tile_picked_unet_relu_e_kernel(tc, xT, w1, w2, skip, offs, cell, out):
         for t in range(PACK):
             nc.sync.dma_start(skip_rows[t][:], skip_view[t])
 
+        ident_f32 = keep.tile([P, P], F32, name="ident_f32")
+        ident_bf16 = keep.tile([P, P], BF16, name="ident_bf16")
+        make_identity(nc, ident_f32[:])
+        make_identity(nc, ident_bf16[:])
+
         up = [keep.tile([P, U], F32, name=f"up{t}") for t in range(PACK)]
         for t in range(PACK):
             nc.vector.memset(up[t][:], 0.0)
@@ -96,10 +102,37 @@ def tile_picked_unet_relu_e_kernel(tc, xT, w1, w2, skip, offs, cell, out):
         nc.scalar.copy(out=w2_grouped[:], in_=w2_raw[:].rearrange("p j c -> p c j"))
 
         z = keep.tile([P, PACK, U], BF16, name="z")
+        BANK = 512
+        blocks = BANK // P
+
+        def turn_onto(bank, rows, half, first):
+            for b in range(blocks):
+                cols = slice(half * BANK + b * P, half * BANK + (b + 1) * P)
+                nc.tensor.matmul(bank[:, b, :], lhsT=rows[:, cols], rhs=ident_f32[:], is_transpose=True,
+                                 start=(first and b == 0), stop=(not first and b == blocks - 1))
+
+        sums = {}
+        for t in range(PACK - 1):
+            for half in range(U // BANK):
+                sums[t, half] = psum.tile([P, blocks, P], F32, name="sums", tag="bank")
+                turn_onto(sums[t, half], skip_rows[t], half, True)
+
+        def add_on_tensor(t):
+            turned = []
+            for half in range(U // BANK):
+                turn_onto(sums[t, half], up[t], half, False)
+                turned.append(keep.tile([P, blocks, P], BF16, name=f"turned{t}_{half}"))
+                nc.scalar.copy(out=turned[half][:], in_=sums[t, half][:])
+            back = psum.tile([P, U // P, P], BF16, name="back", tag="bank")
+            for half in range(U // BANK):
+                for b in range(blocks):
+                    nc.tensor.transpose(back[:, half * blocks + b, :], turned[half][:, b, :], ident_bf16[:])
+            nc.scalar.copy(out=z[:, t, :], in_=back[:].rearrange("p b c -> p (b c)"))
+
         for n, (t, a, b) in enumerate(pieces):
             nc.vector.tensor_copy(up[t][:].indirect(cell_sb[:, a * LIST_COLS : b * LIST_COLS]), h_sb[n][:])
             if b == 2 and t < PACK - 1:
-                nc.gpsimd.tensor_tensor(z[:, t, :], up[t][:], skip_rows[t][:], ADD)
+                add_on_tensor(t)
             if t == 2:
                 quantize(w2_codes[:], w2_scales[:], w2_grouped[:].rearrange("p c j -> p (c j)"))
 

@@ -79,28 +79,29 @@ def tile_picked_unet_relu_e_kernel(tc, xT, w1, w2, skip, offs, cell, out):
         for j in range(PACK):
             for a in range(2):
                 nc.vector.tensor_copy(x_grouped[a][:, :, j], x_rows[j][:].indirect(offs_sb[:, list_halves[a]]))
-                if j == PACK - 1:
-                    quantize(x_codes[:, halves[a]], x_scales[:, halves[a]],
-                             x_grouped[a][:].rearrange("p s j -> p (s j)"))
+        for a, b in ((0, 128), (128, 256), (256, 512)):
+            quantize(x_codes[:, a:b], x_scales[:, a:b],
+                     x_grouped[a // HALF][:, a % HALF : a % HALF + b - a, :].rearrange("p s j -> p (s j)"))
 
         w2_grouped = keep.tile([P, N, PACK], BF16, name="w2_grouped", align_bytes=64)
         w2_codes = keep.tile([P, N], U32, name="w2_codes", align_bytes=64)
         w2_scales = keep.tile([P, N], U8, name="w2_scales", align_bytes=64)
 
-        pieces = [(0, 0, 1), (1, 0, 1), (0, 1, 2), (1, 1, 2), (2, 0, 2), (3, 0, 2)]
+        pieces = [(0, [0, 128]), (1, [0, 128]), (0, [128, 256, 512]), (1, [128, 256, 512]), (2, [0, 512]), (3, [0, 512])]
         h_sb = []
-        for n, (t, a, b) in enumerate(pieces):
-            width = (b - a) * HALF
-            cols = slice(a * HALF, b * HALF)
+        for n, (t, edges) in enumerate(pieces):
+            width = edges[-1] - edges[0]
             rows = slice(t * P, (t + 1) * P)
             acc = psum.tile([P, width], F32, name="acc", tag="bank")
-            product(acc[:], w1_codes[:, rows], w1_scales[:, rows], x_codes[:, cols], x_scales[:, cols])
+            for a, b in zip(edges, edges[1:]):
+                product(acc[:, a - edges[0] : b - edges[0]], w1_codes[:, rows], w1_scales[:, rows], x_codes[:, a:b], x_scales[:, a:b])
             h = keep.tile([P, width], F32, name=f"h{n}")
             nc.scalar.activation(h[:], acc[:], RELU)
             h_sb.append(h)
 
         nc.scalar.copy(out=w2_grouped[:], in_=w2_raw[:].rearrange("p j c -> p c j"))
 
+        quantize(w2_codes[:], w2_scales[:], w2_grouped[:].rearrange("p c j -> p (c j)"))
         z = keep.tile([P, PACK, U], BF16, name="z")
         BANK = 512
         blocks = BANK // P
@@ -121,67 +122,59 @@ def tile_picked_unet_relu_e_kernel(tc, xT, w1, w2, skip, offs, cell, out):
             turned = []
             for half in range(U // BANK):
                 turn_onto(sums[t, half], up[t], half, False)
-                turned.append(keep.tile([P, blocks, P], BF16, name=f"turned{t}_{half}"))
-                nc.scalar.copy(out=turned[half][:], in_=sums[t, half][:])
+                turned.append(z[:, PACK - 1, half * BANK : (half + 1) * BANK].rearrange("p (b c) -> p b c", c=P))
+                nc.scalar.copy(out=turned[half], in_=sums[t, half][:])
             back = psum.tile([P, U // P, P], BF16, name="back", tag="bank")
             for half in range(U // BANK):
                 for b in range(blocks):
                     nc.tensor.transpose(back[:, half * blocks + b, :], turned[half][:, b, :], ident_bf16[:])
             nc.scalar.copy(out=z[:, t, :], in_=back[:].rearrange("p b c -> p (b c)"))
 
-        for n, (t, a, b) in enumerate(pieces):
-            nc.vector.tensor_copy(up[t][:].indirect(cell_sb[:, a * LIST_COLS : b * LIST_COLS]), h_sb[n][:])
-            if b == 2 and t < PACK - 1:
+        for n, (t, edges) in enumerate(pieces):
+            nc.vector.tensor_copy(up[t][:].indirect(cell_sb[:, edges[0] // 16 : edges[-1] // 16]), h_sb[n][:])
+            if edges[-1] == S and t < PACK - 1:
                 add_on_tensor(t)
-            if t == 2:
-                quantize(w2_codes[:], w2_scales[:], w2_grouped[:].rearrange("p c j -> p (c j)"))
 
-        chunks = U // CHUNK
-        z_grouped = [keep.tile([P, CHUNK, PACK], BF16, name=f"z_grouped{c}", align_bytes=64) for c in range(chunks)]
-        z_codes = [keep.tile([P, CHUNK], U32, name=f"z_codes{c}", align_bytes=64) for c in range(chunks)]
-        z_scales = [keep.tile([P, CHUNK], U8, name=f"z_scales{c}", align_bytes=64) for c in range(chunks)]
+        spans = [(0, 128), (128, 384), (768, 1024), (384, 640), (640, 768)]
+        z_grouped = [keep.tile([P, b - a, PACK], BF16, name=f"z_grouped{a}", align_bytes=64) for a, b in spans]
         out_view = out.rearrange("(g p) v -> p g v", p=P)
 
-        def cells(c):
-            return slice(c * CHUNK, (c + 1) * CHUNK)
-
-        def add_last(c):
+        def add_last(a, b):
             t = PACK - 1
-            nc.vector.tensor_tensor(z[:, t, cells(c)], up[t][:, cells(c)], skip_rows[t][:, cells(c)], ADD)
+            nc.vector.tensor_tensor(z[:, t, a:b], up[t][:, a:b], skip_rows[t][:, a:b], ADD)
 
         def interleave(copy, c):
+            a, b = spans[c]
             copy(out=z_grouped[c][:].rearrange("p (c i) t -> p c t i", i=RUN),
-                 in_=z[:, :, cells(c)].rearrange("p t (c i) -> p c t i", i=RUN))
+                 in_=z[:, :, a:b].rearrange("p t (c i) -> p c t i", i=RUN))
 
-        def finish(c):
-            quantize(z_codes[c][:], z_scales[c][:], z_grouped[c][:].rearrange("p v t -> p (v t)"))
-            acc = psum.tile([P, N // P, CHUNK], F32, name="acc", tag="bank")
-            for g in range(N // P):
-                rows = slice(g * P, (g + 1) * P)
-                product(acc[:, g, :], w2_codes[:, rows], w2_scales[:, rows], z_codes[c][:], z_scales[c][:])
-            result = keep.tile([P, N // P, CHUNK], F32, name=f"result{c}")
-            nc.scalar.copy(out=result[:], in_=acc[:])
-            nc.sync.dma_start(out_view[:, :, cells(c)], result[:])
+        def finish(c, copy, queue, banks=1):
+            a, b = spans[c]
+            z_codes = keep.tile([P, b - a], U32, name=f"z_codes{a}", align_bytes=64)
+            z_scales = keep.tile([P, b - a], U8, name=f"z_scales{a}", align_bytes=64)
+            quantize(z_codes[:], z_scales[:], z_grouped[c][:].rearrange("p v t -> p (v t)"))
+            result = keep.tile([P, N // P, b - a], F32, name=f"result{a}")
+            per_bank = N // P // banks
+            for first in range(0, N // P, per_bank):
+                acc = psum.tile([P, per_bank, b - a], F32, name="acc", tag="bank")
+                for g in range(first, first + per_bank):
+                    rows = slice(g * P, (g + 1) * P)
+                    product(acc[:, g - first, :], w2_codes[:, rows], w2_scales[:, rows], z_codes[:], z_scales[:])
+                copy(out=result[:, first : first + per_bank, :], in_=acc[:])
+            queue.dma_start(out_view[:, :, a:b], result[:])
 
-        def finish_last(c):
-            quantize(z_codes[c][:], z_scales[c][:], z_grouped[c][:].rearrange("p v t -> p (v t)"))
-            for g, copy in enumerate((nc.scalar.copy, nc.vector.tensor_copy)):
-                rows = slice(g * P, (g + 1) * P)
-                acc = psum.tile([P, CHUNK], F32, name="acc", tag="bank")
-                product(acc[:], w2_codes[:, rows], w2_scales[:, rows], z_codes[c][:], z_scales[c][:])
-                result = keep.tile([P, CHUNK], F32, name=f"last_result{g}")
-                copy(out=result[:], in_=acc[:])
-                nc.sync.dma_start(out_view[:, g, cells(c)], result[:])
-
-        add_last(0)
+        add_last(0, 128)
         interleave(nc.scalar.copy, 0)
-        add_last(1)
-        add_last(3)
-        interleave(nc.scalar.copy, 3)
-        add_last(2)
+        add_last(768, 1024)
+        interleave(nc.scalar.copy, 2)
+        add_last(128, 384)
+        add_last(384, 640)
+        add_last(640, 768)
+        interleave(nc.scalar.copy, 4)
         interleave(nc.vector.tensor_copy, 1)
-        finish(0)
-        finish(1)
-        interleave(nc.vector.tensor_copy, 2)
-        finish(3)
-        finish_last(2)
+        finish(0, nc.scalar.copy, nc.sync)
+        finish(1, nc.scalar.copy, nc.sync)
+        interleave(nc.vector.tensor_copy, 3)
+        finish(2, nc.scalar.copy, nc.sync)
+        finish(3, nc.vector.tensor_copy, nc.sync, banks=2)
+        finish(4, nc.scalar.copy, nc.scalar)

from contextlib import ExitStack

import concourse.mybir as mybir
from concourse.masks import make_identity

K, T, S, H, N, U = 512, 2048, 512, 512, 256, 1024
FLOPS = 2 * K * H * S + 2 * H * N * U

F32 = mybir.dt.float32
BF16 = mybir.dt.bfloat16
U32 = mybir.dt.uint32
U16 = mybir.dt.uint16
U8 = mybir.dt.uint8
FP8X4 = mybir.dt.float8_e4m3fn_x4
RELU = mybir.ActivationFunctionType.Relu
ADD = mybir.AluOpType.add

P = 128
PACK = 4
HALF = S // 2
LIST_COLS = HALF // 16
CHUNK = 256
RUN = 4


def tile_picked_unet_relu_e_kernel(tc, xT, w1, w2, skip, offs, cell, out):
    nc = tc.nc

    def quantize(codes, scales, grouped):
        nc.vector.quantize_mx(out=codes.bitcast(FP8X4), scales=scales, in_=grouped)

    def product(acc, w_codes, w_scales, v_codes, v_scales):
        nc.tensor.matmul_mx(out=acc, lhsT=w_codes.bitcast(FP8X4), lhsT_scale=w_scales,
                            rhs=v_codes.bitcast(FP8X4), rhs_scale=v_scales, start=True, stop=True)

    with ExitStack() as ctx:
        keep = ctx.enter_context(tc.tile_pool(name="keep", bufs=1))
        psum = ctx.enter_context(tc.psum_pool(name="psum", bufs=8))

        offs_sb = keep.tile([P, S // 16], U16, name="offs_sb")
        cell_sb = keep.tile([P, S // 16], U16, name="cell_sb")
        w1_raw = keep.tile([P, PACK, H], F32, name="w1_raw")
        w2_raw = keep.tile([P, PACK, N], F32, name="w2_raw")
        x_rows = [keep.tile([P, T], F32, name=f"x_rows{j}") for j in range(PACK)]
        skip_rows = [keep.tile([P, U], F32, name=f"skip_rows{t}") for t in range(PACK)]
        x_view = xT.rearrange("(p j) w -> j p w", j=PACK)
        skip_view = skip.rearrange("(p t) v -> t p v", t=PACK)

        nc.sync.dma_start(w1_raw[:], w1.rearrange("(p j) c -> p j c", j=PACK))
        nc.sync.dma_start(offs_sb[:], offs)
        for j in range(PACK):
            nc.sync.dma_start(x_rows[j][:], x_view[j])
        nc.sync.dma_start(cell_sb[:], cell)
        nc.sync.dma_start(w2_raw[:], w2.rearrange("(p j) c -> p j c", j=PACK))
        for t in range(PACK):
            nc.sync.dma_start(skip_rows[t][:], skip_view[t])

        ident_f32 = keep.tile([P, P], F32, name="ident_f32")
        ident_bf16 = keep.tile([P, P], BF16, name="ident_bf16")
        make_identity(nc, ident_f32[:])
        make_identity(nc, ident_bf16[:])

        up = [keep.tile([P, U], F32, name=f"up{t}") for t in range(PACK)]
        for t in range(PACK):
            nc.vector.memset(up[t][:], 0.0)

        w1_grouped = keep.tile([P, PACK * H], BF16, name="w1_grouped", align_bytes=64)
        w1_codes = keep.tile([P, H], U32, name="w1_codes", align_bytes=64)
        w1_scales = keep.tile([P, H], U8, name="w1_scales", align_bytes=64)
        nc.scalar.copy(out=w1_grouped[:].rearrange("p (t m j) -> p t m j", t=PACK, j=PACK),
                       in_=w1_raw[:].rearrange("p j (m t) -> p t m j", t=PACK))
        quantize(w1_codes[:], w1_scales[:], w1_grouped[:])

        x_grouped = [keep.tile([P, HALF, PACK], BF16, name=f"x_grouped{a}", align_bytes=64) for a in range(2)]
        x_codes = keep.tile([P, S], U32, name="x_codes", align_bytes=64)
        x_scales = keep.tile([P, S], U8, name="x_scales", align_bytes=64)
        halves = [slice(a * HALF, (a + 1) * HALF) for a in range(2)]
        list_halves = [slice(a * LIST_COLS, (a + 1) * LIST_COLS) for a in range(2)]
        for j in range(PACK):
            for a in range(2):
                nc.vector.tensor_copy(x_grouped[a][:, :, j], x_rows[j][:].indirect(offs_sb[:, list_halves[a]]))
        for a, b in ((0, 128), (128, 256), (256, 512)):
            quantize(x_codes[:, a:b], x_scales[:, a:b],
                     x_grouped[a // HALF][:, a % HALF : a % HALF + b - a, :].rearrange("p s j -> p (s j)"))

        w2_grouped = keep.tile([P, N, PACK], BF16, name="w2_grouped", align_bytes=64)
        w2_codes = keep.tile([P, N], U32, name="w2_codes", align_bytes=64)
        w2_scales = keep.tile([P, N], U8, name="w2_scales", align_bytes=64)

        pieces = [(0, [0, 128]), (1, [0, 128]), (0, [128, 256, 512]), (1, [128, 256, 512]), (2, [0, 512]), (3, [0, 512])]
        h_sb = []
        for n, (t, edges) in enumerate(pieces):
            width = edges[-1] - edges[0]
            rows = slice(t * P, (t + 1) * P)
            acc = psum.tile([P, width], F32, name="acc", tag="bank")
            for a, b in zip(edges, edges[1:]):
                product(acc[:, a - edges[0] : b - edges[0]], w1_codes[:, rows], w1_scales[:, rows], x_codes[:, a:b], x_scales[:, a:b])
            h = keep.tile([P, width], F32, name=f"h{n}")
            nc.scalar.activation(h[:], acc[:], RELU)
            h_sb.append(h)

        nc.scalar.copy(out=w2_grouped[:], in_=w2_raw[:].rearrange("p j c -> p c j"))

        quantize(w2_codes[:], w2_scales[:], w2_grouped[:].rearrange("p c j -> p (c j)"))
        z = keep.tile([P, PACK, U], BF16, name="z")
        BANK = 512
        blocks = BANK // P

        def turn_onto(bank, rows, half, first):
            for b in range(blocks):
                cols = slice(half * BANK + b * P, half * BANK + (b + 1) * P)
                nc.tensor.matmul(bank[:, b, :], lhsT=rows[:, cols], rhs=ident_f32[:], is_transpose=True,
                                 start=(first and b == 0), stop=(not first and b == blocks - 1))

        sums = {}
        for t in range(PACK - 1):
            for half in range(U // BANK):
                sums[t, half] = psum.tile([P, blocks, P], F32, name="sums", tag="bank")
                turn_onto(sums[t, half], skip_rows[t], half, True)

        def add_on_tensor(t):
            turned = []
            for half in range(U // BANK):
                turn_onto(sums[t, half], up[t], half, False)
                turned.append(z[:, PACK - 1, half * BANK : (half + 1) * BANK].rearrange("p (b c) -> p b c", c=P))
                nc.scalar.copy(out=turned[half], in_=sums[t, half][:])
            back = psum.tile([P, U // P, P], BF16, name="back", tag="bank")
            for half in range(U // BANK):
                for b in range(blocks):
                    nc.tensor.transpose(back[:, half * blocks + b, :], turned[half][:, b, :], ident_bf16[:])
            nc.scalar.copy(out=z[:, t, :], in_=back[:].rearrange("p b c -> p (b c)"))

        for n, (t, edges) in enumerate(pieces):
            nc.vector.tensor_copy(up[t][:].indirect(cell_sb[:, edges[0] // 16 : edges[-1] // 16]), h_sb[n][:])
            if edges[-1] == S and t < PACK - 1:
                add_on_tensor(t)

        spans = [(0, 128), (128, 384), (768, 1024), (384, 640), (640, 768)]
        z_grouped = [keep.tile([P, b - a, PACK], BF16, name=f"z_grouped{a}", align_bytes=64) for a, b in spans]
        out_view = out.rearrange("(g p) v -> p g v", p=P)

        def add_last(a, b):
            t = PACK - 1
            nc.vector.tensor_tensor(z[:, t, a:b], up[t][:, a:b], skip_rows[t][:, a:b], ADD)

        def interleave(copy, c):
            a, b = spans[c]
            copy(out=z_grouped[c][:].rearrange("p (c i) t -> p c t i", i=RUN),
                 in_=z[:, :, a:b].rearrange("p t (c i) -> p c t i", i=RUN))

        def finish(c, copy, queue, banks=1):
            a, b = spans[c]
            z_codes = keep.tile([P, b - a], U32, name=f"z_codes{a}", align_bytes=64)
            z_scales = keep.tile([P, b - a], U8, name=f"z_scales{a}", align_bytes=64)
            quantize(z_codes[:], z_scales[:], z_grouped[c][:].rearrange("p v t -> p (v t)"))
            result = keep.tile([P, N // P, b - a], F32, name=f"result{a}")
            per_bank = N // P // banks
            for first in range(0, N // P, per_bank):
                acc = psum.tile([P, per_bank, b - a], F32, name="acc", tag="bank")
                for g in range(first, first + per_bank):
                    rows = slice(g * P, (g + 1) * P)
                    product(acc[:, g - first, :], w2_codes[:, rows], w2_scales[:, rows], z_codes[:], z_scales[:])
                copy(out=result[:, first : first + per_bank, :], in_=acc[:])
            queue.dma_start(out_view[:, :, a:b], result[:])

        add_last(0, 128)
        interleave(nc.scalar.copy, 0)
        add_last(768, 1024)
        interleave(nc.scalar.copy, 2)
        add_last(128, 384)
        add_last(384, 640)
        add_last(640, 768)
        interleave(nc.scalar.copy, 4)
        interleave(nc.vector.tensor_copy, 1)
        finish(0, nc.scalar.copy, nc.sync)
        finish(1, nc.scalar.copy, nc.sync)
        interleave(nc.vector.tensor_copy, 3)
        finish(2, nc.scalar.copy, nc.sync)
        finish(3, nc.vector.tensor_copy, nc.sync, banks=2)
        finish(4, nc.scalar.copy, nc.scalar)
